import numpy as np
import ml_dtypes


def mxq(x, axis, fmt="e4m3"):
    dtype, down = {"e4m3": (ml_dtypes.float8_e4m3fn, 7), "e5m2": (ml_dtypes.float8_e5m2, 14)}[fmt]
    v = np.moveaxis(np.asarray(x, np.float32).astype(ml_dtypes.bfloat16).astype(np.float64), axis, -1)
    blocks = v.reshape(v.shape[:-1] + (-1, 32))
    amax = np.abs(blocks).max(-1, keepdims=True)
    byte = np.maximum(np.where(amax > 0, np.frexp(amax)[1] - 1 + 127, 0) - down, 1)
    scale = np.exp2(byte - 127.0)
    codes = (blocks / scale).astype(np.float32).astype(dtype).astype(np.float64)
    return np.moveaxis((codes * scale).reshape(v.shape), -1, axis)


WIDE = False


def mx_kscale(k):
    if not WIDE:
        return np.ones(k)
    levels = np.array([10, -10, 5, -5, 0])
    if k % 512:
        return np.exp2(np.random.permutation(np.resize(levels, k // 32))).repeat(32)
    a = np.empty((k // 512, 16))
    for p in range(k // 512):
        a[p, :8] = np.random.permutation(np.resize(levels, 8))
        for g in range(8):
            far = levels[np.abs(levels - a[p, g]) >= 10]
            a[p, g + 8] = far[np.random.randint(len(far))]
    return np.exp2(a.ravel()).repeat(32)


def f64(x):
    return np.asarray(x).astype(np.float64)


def striped(idx):
    return np.tile(idx.reshape(-1, 16).T, (8, 1)).astype(np.uint16)


def unstriped(offs):
    return offs[:16].T.reshape(-1).astype(np.int64)


def striped8(idx):
    return np.concatenate([x.reshape(-1, 16).T for x in idx]).astype(np.uint16)


def runs(offs, k):
    lists = np.stack([offs[16 * r : 16 * r + 16].T.reshape(-1) for r in range(8)]).astype(np.int64)
    return lists[np.arange(k) % 512 // 64]


def pack_weight(w):
    k, n = w.shape
    w = f64(np.asarray(w, np.float32).astype(ml_dtypes.bfloat16)).reshape(k // 32, 32, n)
    amax = np.abs(w).max(1)
    byte = np.clip(np.where(amax > 0, np.frexp(amax)[1] - 1 + 127 - 7, 1), 1, 254)
    scaled = (w * np.exp2(127.0 - byte)[:, None, :]).reshape(k, n).astype(np.float32)
    words = np.ascontiguousarray(scaled.reshape(k // 512, 128, 4, n).transpose(0, 1, 3, 2)).astype(ml_dtypes.float8_e4m3fn).view(np.uint8)
    return words, np.ascontiguousarray(byte.astype(np.uint8).reshape(k // 512, 16, n))


def unpack_weight(words, scales):
    g, p, n, _ = words.shape
    vals = np.ascontiguousarray(words).view(ml_dtypes.float8_e4m3fn).astype(np.float64) * np.repeat(np.exp2(scales.astype(np.float64) - 127.0), 8, axis=1)[..., None]
    return vals.transpose(0, 1, 3, 2).reshape(g * 512, n)


E2M1 = np.array([0.0, 0.5, 1.0, 1.5, 2.0, 3.0, 4.0, 6.0, -0.0, -0.5, -1.0, -1.5, -2.0, -3.0, -4.0, -6.0])


def pack_fp4(w):
    k, n = w.shape
    w = f64(np.asarray(w, np.float32).astype(ml_dtypes.bfloat16)).reshape(k // 32, 32, n)
    amax = np.abs(w).max(1)
    mant, ex = np.frexp(amax / 6.0)
    byte = np.clip(np.where(amax > 0, np.where(mant > 0.5, ex, ex - 1) + 127, 1), 1, 254)
    scaled = (w * np.exp2(127.0 - byte)[:, None, :]).reshape(k, n).astype(np.float32)
    c = np.ascontiguousarray(scaled.reshape(k // 512, 128, 4, n).transpose(0, 1, 3, 2)).astype(ml_dtypes.float4_e2m1fn).view(np.uint8) & 0xF
    words = (c[..., 0::2] | (c[..., 1::2] << 4)).reshape(k // 512, 128, 2 * n)
    return np.ascontiguousarray(words), np.ascontiguousarray(byte.astype(np.uint8).reshape(k // 512, 16, n))


def unpack_fp4(words, scales):
    g, _, n = scales.shape
    words = np.ascontiguousarray(words).reshape(g, 128, n, 2)
    nib = np.empty((g, 128, n, 4), np.uint8)
    nib[..., 0::2] = words & 0xF
    nib[..., 1::2] = words >> 4
    vals = E2M1[nib] * np.repeat(np.exp2(scales.astype(np.float64) - 127.0), 8, axis=1)[..., None]
    return vals.transpose(0, 1, 3, 2).reshape(g * 512, n)


def planes(y):
    n, m = y.shape
    v = y.astype(np.float32).astype(ml_dtypes.bfloat16).astype(np.float64).reshape(n // 32, 32, m)
    top = np.abs(v).max(1)
    byte = np.clip(np.where(top > 0, np.frexp(top)[1] - 1 + 127 - 7, 1), 1, 254)
    codes = (v * np.exp2(127.0 - byte)[:, None, :]).reshape(n, m).astype(np.float32).astype(ml_dtypes.float8_e4m3fn).view(np.uint8)
    words = codes.reshape(n // 512, 128, 4, m).transpose(0, 1, 3, 2)
    return np.ascontiguousarray(words), np.ascontiguousarray(byte.astype(np.uint8).reshape(n // 512, 16, m))


K, T, S, N, G, H, J = 512, 2048, 512, 512, 2048, 512, 512


def setup_inputs():
    n = np.random.standard_normal
    s = mx_kscale(K)[:, None]
    u = mx_kscale(S)
    packed_xT = pack_weight(n((K, T)) * s)
    packed_dT = pack_weight(n((K, G)) / s)
    packed_w1 = pack_fp4(n((H, N)) / np.sqrt(H) / u[:, None])
    return {
        "x_words": packed_xT[0],
        "x_scales": packed_xT[1],
        "d_words": packed_dT[0],
        "d_scales": packed_dT[1],
        "gn": (np.random.uniform(0.5, 1.5, (H, 1)) * u[:, None]).astype(np.float32),
        "w1_words": packed_w1[0],
        "w1_scales": packed_w1[1],
        "tab": n((N, J)).astype(np.float32),
        "offs": striped(np.random.permutation(T)[:S]),
        "kidx": striped8(np.random.randint(0, G, (8, H))),
        "n1": striped8(np.stack([np.random.permutation(S) for _ in range(8)])),
        "n2": striped8(np.stack([np.random.permutation(S) for _ in range(8)])),
        "n3": striped8(np.random.randint(0, J, (8, S))),
        "n4": striped8(np.random.randint(0, J, (8, S))),
        "n5": striped8(np.stack([np.random.permutation(S) for _ in range(8)])),
    }


def reference(x_words, x_scales, d_words, d_scales, gn, w1_words, w1_scales, tab, offs, kidx, n1, n2, n3, n4, n5):
    d_kidx = unpack_weight(d_words, d_scales)[np.arange(K)[:, None], runs(kidx, K)]
    xq = unpack_weight(x_words, x_scales)[:, unstriped(offs)]
    s = 0.0625 * (d_kidx.T @ xq)
    ex = np.exp(0.5 * s)
    z = f64(gn) * ((2.0 * ex) / (ex + ex[np.arange(H)[:, None], runs(n1, H)] + ex[np.arange(H)[:, None], runs(n2, H)]))
    h = unpack_fp4(w1_words, w1_scales).T @ mxq(z, 0, "e4m3")
    out_0 = (h[np.arange(N)[:, None], runs(n5, N)]) * (f64(tab)[np.arange(N)[:, None], runs(n3, N)]) + f64(tab)[np.arange(N)[:, None], runs(n4, N)]
    return (out_0,) + planes(out_0)

@@ -1,0 +1,194 @@
+from contextlib import ExitStack
+
+import concourse.mybir as mybir
+
+F32 = mybir.dt.float32
+BF16 = mybir.dt.bfloat16
+I32 = mybir.dt.int32
+U32 = mybir.dt.uint32
+U16 = mybir.dt.uint16
+U8 = mybir.dt.uint8
+FP8X4 = mybir.dt.float8_e4m3fn_x4
+FP4X4 = mybir.dt.float4_e2m1fn_x4
+ACT = mybir.ActivationFunctionType
+MULT = mybir.AluOpType.mult
+ADD = mybir.AluOpType.add
+
+P = 128
+T = 2048
+S = 512
+FLOPS = 2 * 2 * 512 * 512 * 512
+SCALAR_TILES = (2, 3)
+
+
+def tile_picked_keysharekinda_none_po_kernel(
+    tc, x_words, x_scales, d_words, d_scales, gn, w1_words, w1_scales, tab, offs, kidx, n1, n2, n3, n4, n5, out_0, out_1, out_2
+):
+    nc = tc.nc
+    with ExitStack() as ctx:
+        keep = ctx.enter_context(tc.tile_pool(name="keep", bufs=1))
+        shared = ctx.enter_context(tc.tile_pool(name="shared", bufs=1))
+        psum = ctx.enter_context(tc.psum_pool(name="psum", bufs=1))
+
+        def sb(name, shape, dtype):
+            return keep.tile(shape, dtype, name=name, align_bytes=64)
+
+        def load_list(name, src):
+            lst = sb(name, [P, S // 16], U16)
+            nc.sync.dma_start(lst[:], src)
+            return lst
+
+        def entries(lst, lo, hi):
+            return lst[:, lo // 16 : hi // 16]
+
+        warm = sb("warm", [P, 1], F32)
+        warm2 = sb("warm2", [P, 1], F32)
+        nc.gpsimd.memset(warm[:], 0.0)
+        nc.scalar.activation(warm2[:], warm[:], ACT.Exp)
+
+        ds_win = sb("ds_win", [P, T], U8)
+        xs_win = sb("xs_win", [P, T], U8)
+        nc.vector.memset(ds_win[:].bitcast(I32), 0)
+        nc.vector.memset(xs_win[:].bitcast(I32), 0)
+        kidx_t = load_list("kidx_t", kidx)
+        for e in range(2):
+            nc.scalar.dma_start(ds_win[e:P:16, :].bitcast(I32), d_scales[0].bitcast(I32)[e:16:2, :])
+        dw_win = shared.tile([P, T], I32, name="dw_win", offset=0)
+        nc.sync.dma_start(dw_win[:], d_words[0].rearrange("p n t -> p (n t)").bitcast(I32))
+        offs_t = load_list("offs_t", offs)
+        n1_t = load_list("n1_t", n1)
+        n2_t = load_list("n2_t", n2)
+        xw_win = shared.tile([P, T], I32, name="xw_win", offset=4 * T)
+        nc.sync.dma_start(xw_win[:], x_words[0].rearrange("p n t -> p (n t)").bitcast(I32))
+        n3_t = load_list("n3_t", n3)
+        n5_t = load_list("n5_t", n5)
+        n4_t = load_list("n4_t", n4)
+        for r in range(4):
+            nc.gpsimd.dma_start(xs_win[r:P:32, :].bitcast(I32), x_scales[0].bitcast(I32)[r:16:4, :])
+        g_raw = sb("g_raw", [P, 4], F32)
+        nc.gpsimd.dma_start(g_raw[:], gn.rearrange("(p t) o -> p (t o)", t=4))
+        ww_raw = sb("ww_raw", [P, 2 * S], U8)
+        nc.gpsimd.dma_start(ww_raw[:].bitcast(I32), w1_words[0].bitcast(I32))
+
+        ds_got = sb("ds_got", [P, S], U8)
+        nc.vector.tensor_copy(ds_got[:], ds_win[:].indirect(kidx_t[:]))
+        ds = sb("ds", [P, S], U8)
+        nc.vector.tensor_copy(ds[:].rearrange("p (t m) -> p t m", t=4), ds_got[:].rearrange("p (m t) -> p t m", t=4))
+        for e in range(2):
+            nc.scalar.dma_start(ds[2 + e : P : 32, :].bitcast(I32), ds[16 + e : P : 32, :].bitcast(I32))
+        dw_got = sb("dw_got", [P, S], U32)
+        nc.vector.tensor_copy(dw_got[:], dw_win[:].bitcast(U32).indirect(kidx_t[:]))
+        dw = sb("dw", [P, S], U32)
+        nc.vector.tensor_copy(dw[:].rearrange("p (t m) -> p t m", t=4), dw_got[:].rearrange("p (m t) -> p t m", t=4))
+        xs = sb("xs", [P, S], U8)
+        nc.vector.tensor_copy(xs[:], xs_win[:].indirect(offs_t[:]))
+        xw = sb("xw", [P, S], U32)
+        nc.vector.tensor_copy(xw[:], xw_win[:].bitcast(U32).indirect(offs_t[:]))
+
+        tabs = []
+        for t in range(4):
+            tab_t = shared.tile([P, S], F32, name="tab%d" % t, offset=4 * S * t)
+            nc.sync.dma_start(tab_t[:], tab.rearrange("(p t) c -> p t c", t=4)[:, t, :])
+            tabs.append(tab_t)
+        ws_raw = shared.tile([P, S], U8, name="ws_raw", offset=4 * T)
+        nc.gpsimd.memset(ws_raw[:].bitcast(I32), 0)
+        for r in range(4):
+            nc.sync.dma_start(ws_raw[r:P:32, :].bitcast(I32), w1_scales[0].bitcast(I32)[r:16:4, :])
+
+        halves = [(0, 256), (256, 512)]
+        den = sb("den", [P, 4, S], F32)
+        num = sb("num", [P, 4, S], F32)
+        g2 = sb("g2", [P, 4], F32)
+        nc.vector.tensor_scalar(g2[:], g_raw[:], 2.0, None, MULT)
+        banks = []
+        for t in range(4):
+            bank = psum.tile([P, S], F32, name="s%d" % t)
+            cols = slice(t * P, (t + 1) * P)
+            nc.tensor.matmul_mx(bank[:], lhsT=dw[:, cols].bitcast(FP8X4), lhsT_scale=ds[:, cols],
+                                rhs=xw[:].bitcast(FP8X4), rhs_scale=xs[:], start=True, stop=True)
+            banks.append(bank)
+        exs = []
+        for t in range(4):
+            ex = sb("ex%d" % t, [P, S], F32)
+            other = sb("other%d" % t, [P, S], F32)
+            nc.scalar.activation(ex[:], banks[t][:], ACT.Exp, scale=0.03125)
+            if t in SCALAR_TILES:
+                nc.scalar.copy(other[:], banks[t][:])
+            else:
+                nc.scalar.activation(other[:], banks[t][:], ACT.Exp, scale=0.03125)
+            exs.append((ex, other))
+        for t in range(4):
+            ex, other = exs[t]
+            part = sb("part%d" % t, [P, S], F32)
+            if t in SCALAR_TILES:
+                e1 = sb("e1_%d" % t, [P, S], F32)
+                e2 = sb("e2_%d" % t, [P, S], F32)
+                for lo, hi in halves:
+                    nc.scalar.activation(e1[:, lo:hi], other[:].indirect(entries(n1_t, lo, hi)), ACT.Exp, scale=0.03125)
+                    nc.scalar.activation(e2[:, lo:hi], other[:].indirect(entries(n2_t, lo, hi)), ACT.Exp, scale=0.03125)
+                    nc.vector.tensor_tensor(part[:, lo:hi], e1[:, lo:hi], ex[:, lo:hi], ADD)
+                    nc.vector.tensor_tensor(den[:, t, lo:hi], part[:, lo:hi], e2[:, lo:hi], ADD)
+            else:
+                for lo, hi in halves:
+                    nc.vector.tensor_tensor(part[:, lo:hi], ex[:].indirect(entries(n1_t, lo, hi)), other[:, lo:hi], ADD)
+                for lo, hi in halves:
+                    nc.vector.tensor_tensor(den[:, t, lo:hi], ex[:].indirect(entries(n2_t, lo, hi)), part[:, lo:hi], ADD)
+            nc.vector.tensor_scalar(num[:, t, :], ex[:], g2[:, t : t + 1], None, MULT)
+
+        ww = sb("ww", [P, 2 * S], U8)
+        nc.vector.tensor_copy(ww[:].rearrange("p (t m b) -> p t m b", t=4, b=2), ww_raw[:].rearrange("p (m t b) -> p t m b", t=4, b=2))
+        ws = sb("ws", [P, S], U8)
+        nc.vector.tensor_copy(ws[:].rearrange("p (t m) -> p t m", t=4), ws_raw[:].rearrange("p (m t) -> p t m", t=4))
+
+        gain = sb("gain", [P, 4, S], F32)
+        for t in range(4):
+            for lo, hi in halves:
+                nc.vector.tensor_copy(gain[:, t, lo:hi], tabs[t][:].indirect(entries(n3_t, lo, hi)))
+
+        hbanks = [psum.tile([P, S], F32, name="h%d" % t) for t in range(4)]
+        zw = sb("zw", [P, S], U32)
+        zs = sb("zs", [P, S], U8)
+        for c in range(4):
+            cols = slice(c * P, (c + 1) * P)
+            root = sb("root%d" % c, [P, 4, P], F32)
+            inv = sb("inv%d" % c, [P, 4, P], F32)
+            nc.scalar.activation(root[:], den[:, :, cols], ACT.Abs_reciprocal_sqrt)
+            nc.scalar.activation(inv[:], root[:], ACT.Square)
+            z = sb("z%d" % c, [P, 4 * P], BF16)
+            nc.vector.tensor_tensor(
+                z[:].rearrange("p (b i t) -> p b t i", i=4, t=4),
+                num[:, :, cols].rearrange("p t (b i) -> p b t i", i=4),
+                inv[:].rearrange("p t (b i) -> p b t i", i=4),
+                MULT,
+            )
+            nc.vector.quantize_mx(out=zw[:, cols].bitcast(FP8X4), scales=zs[:, cols], in_=z[:])
+            for t in range(4):
+                nc.tensor.matmul_mx(hbanks[t][:, cols], lhsT=ww[:, 2 * P * t : 2 * P * (t + 1)].bitcast(FP4X4),
+                                    lhsT_scale=ws[:, P * t : P * (t + 1)], rhs=zw[:, cols].bitcast(FP8X4),
+                                    rhs_scale=zs[:, cols], start=True, stop=True)
+        hs = []
+        for t in range(4):
+            h = sb("hs%d" % t, [P, S], F32)
+            nc.scalar.copy(h[:], hbanks[t][:])
+            hs.append(h)
+
+        ow = sb("ow", [P, S], I32)
+        osc = sb("osc", [P, S], U8)
+        out_rows = out_0.rearrange("(p t) c -> p t c", t=4)
+        out_words = out_1[0].rearrange("p n t -> p (n t)").bitcast(I32)
+        for k, (lo, hi) in enumerate([(0, 256), (256, 384), (384, 512)]):
+            n = hi - lo
+            prod = sb("prod%d" % k, [P, 4, n], F32)
+            res = sb("res%d" % k, [P, 4, n], F32)
+            for t in range(4):
+                nc.vector.tensor_tensor(prod[:, t, :], hs[t][:].indirect(entries(n5_t, lo, hi)), gain[:, t, lo:hi], MULT)
+            for t in range(4):
+                nc.vector.tensor_tensor(res[:, t, :], tabs[t][:].indirect(entries(n4_t, lo, hi)), prod[:, t, :], ADD)
+            nc.sync.dma_start(out_rows[:, :, lo:hi], res[:])
+            rb = sb("rb%d" % k, [P, 4 * n], BF16)
+            nc.scalar.copy(rb[:].rearrange("p (b i t) -> p b t i", i=4, t=4), res[:].rearrange("p t (b i) -> p b t i", i=4))
+            nc.vector.quantize_mx(out=ow[:, lo:hi].bitcast(FP8X4), scales=osc[:, lo:hi], in_=rb[:])
+            nc.sync.dma_start(out_words[:, lo:hi], ow[:, lo:hi])
+        for r in range(4):
+            queue = nc.scalar if r % 2 else nc.sync
+            queue.dma_start(out_2[0].bitcast(I32)[r:16:4, :], osc[r:P:32, :].bitcast(I32))

@@ -1,6 +1,7 @@
 from contextlib import ExitStack
 
 import concourse.mybir as mybir
+from concourse.masks import make_identity
 
 F32 = mybir.dt.float32
 BF16 = mybir.dt.bfloat16
@@ -15,10 +16,21 @@ MULT = mybir.AluOpType.mult
 ADD = mybir.AluOpType.add
 
 P = 128
-T = 2048
+TILES = 4
+TABLE = 2048
 S = 512
-FLOPS = 2 * 2 * 512 * 512 * 512
+BLOCKS = 16
+FLOPS = 2 * 2 * S * S * S
+EXP_SCALE = 0.0625 * 0.5
+HALVES = ((0, S // 2), (S // 2, S))
+VECTOR_TILES = (0, 1)
 SCALAR_TILES = (2, 3)
+OUT_CHUNKS = ((0, 256), (256, 384), (384, 512))
+D_WORDS_AT = 0
+X_WORDS_AT = 4 * TABLE
+W1_SCALES_AT = 8 * TABLE - S
+W1_WORDS_AT = W1_SCALES_AT - 2 * S
+TAB_AT = W1_WORDS_AT - TILES * 4 * S
 
 
 def tile_picked_keysharekinda_none_po_kernel(
@@ -27,168 +39,214 @@ def tile_picked_keysharekinda_none_po_kernel(
     nc = tc.nc
     with ExitStack() as ctx:
         keep = ctx.enter_context(tc.tile_pool(name="keep", bufs=1))
-        shared = ctx.enter_context(tc.tile_pool(name="shared", bufs=1))
+        reused = ctx.enter_context(tc.tile_pool(name="reused", bufs=1))
         psum = ctx.enter_context(tc.psum_pool(name="psum", bufs=1))
 
-        def sb(name, shape, dtype):
-            return keep.tile(shape, dtype, name=name, align_bytes=64)
+        def sbuf(name, shape, dtype, tag=None):
+            return keep.tile(shape, dtype, name=name, tag=tag or name, align_bytes=64)
 
         def load_list(name, src):
-            lst = sb(name, [P, S // 16], U16)
+            lst = sbuf(name, [P, S // 16], U16)
             nc.sync.dma_start(lst[:], src)
             return lst
 
         def entries(lst, lo, hi):
             return lst[:, lo // 16 : hi // 16]
 
-        warm = sb("warm", [P, 1], F32)
-        warm2 = sb("warm2", [P, 1], F32)
-        nc.gpsimd.memset(warm[:], 0.0)
-        nc.scalar.activation(warm2[:], warm[:], ACT.Exp)
+        def load_scale_table(name, scales):
+            win = sbuf(name, [P, TABLE], U8)
+            rows = scales[0].bitcast(I32).unsqueeze(1).to_broadcast([BLOCKS, P // BLOCKS, TABLE // 4])
+            nc.sync.dma_start(win[:].bitcast(I32), rows)
+            return win
 
-        ds_win = sb("ds_win", [P, T], U8)
-        xs_win = sb("xs_win", [P, T], U8)
-        nc.vector.memset(ds_win[:].bitcast(I32), 0)
-        nc.vector.memset(xs_win[:].bitcast(I32), 0)
+        def load_word_table(name, words, at):
+            win = reused.tile([P, TABLE], I32, name=name, offset=at)
+            nc.sync.dma_start(win[:], words[0].rearrange("p n t -> p (n t)").bitcast(I32))
+            return win
+
+        def by_lines(tiles):
+            return tiles.rearrange("p t (b i) -> p b t i", i=4)
+
+        def interleaved(flat):
+            return flat.rearrange("p (b i t) -> p b t i", i=4, t=TILES)
+
+        ex_wins = [sbuf("ex_win%d" % t, [P, 2 * S], F32) for t in VECTOR_TILES]
+        nc.vector.memset(ex_wins[0][:, S:], 0.0)
+        nc.scalar.activation(ex_wins[1][:, S:], ex_wins[0][:, S:], ACT.Exp)
+        raw_wins = {t: sbuf("raw_win%d" % t, [P, 2 * S], F32) for t in SCALAR_TILES}
+        h_wins = [sbuf("h_win%d" % t, [P, 2 * S], F32) for t in range(TILES)]
+        ex = [ex_wins[t][:, :S] for t in VECTOR_TILES] + [raw_wins[t][:, S:] for t in SCALAR_TILES]
+        ident = sbuf("ident", [P, P], F32)
+        make_identity(nc, ident[:])
+
         kidx_t = load_list("kidx_t", kidx)
-        for e in range(2):
-            nc.scalar.dma_start(ds_win[e:P:16, :].bitcast(I32), d_scales[0].bitcast(I32)[e:16:2, :])
-        dw_win = shared.tile([P, T], I32, name="dw_win", offset=0)
-        nc.sync.dma_start(dw_win[:], d_words[0].rearrange("p n t -> p (n t)").bitcast(I32))
+        d_scale_win = load_scale_table("d_scale_win", d_scales)
         offs_t = load_list("offs_t", offs)
+        x_scale_win = load_scale_table("x_scale_win", x_scales)
         n1_t = load_list("n1_t", n1)
         n2_t = load_list("n2_t", n2)
-        xw_win = shared.tile([P, T], I32, name="xw_win", offset=4 * T)
-        nc.sync.dma_start(xw_win[:], x_words[0].rearrange("p n t -> p (n t)").bitcast(I32))
+        d_word_win = load_word_table("d_word_win", d_words, D_WORDS_AT)
+        x_word_win = load_word_table("x_word_win", x_words, X_WORDS_AT)
         n3_t = load_list("n3_t", n3)
         n5_t = load_list("n5_t", n5)
         n4_t = load_list("n4_t", n4)
-        for r in range(4):
-            nc.gpsimd.dma_start(xs_win[r:P:32, :].bitcast(I32), x_scales[0].bitcast(I32)[r:16:4, :])
-        g_raw = sb("g_raw", [P, 4], F32)
-        nc.gpsimd.dma_start(g_raw[:], gn.rearrange("(p t) o -> p (t o)", t=4))
-        ww_raw = sb("ww_raw", [P, 2 * S], U8)
-        nc.gpsimd.dma_start(ww_raw[:].bitcast(I32), w1_words[0].bitcast(I32))
+        gain = sbuf("gain", [P, TILES], F32)
+        nc.sync.dma_start(gain[:], gn.rearrange("(p t) o -> p (t o)", t=TILES))
+        w1_word_raw = sbuf("w1_word_raw", [P, 2 * S], U8)
+        nc.gpsimd.dma_start(w1_word_raw[:].bitcast(I32), w1_words[0].bitcast(I32))
 
-        ds_got = sb("ds_got", [P, S], U8)
-        nc.vector.tensor_copy(ds_got[:], ds_win[:].indirect(kidx_t[:]))
-        ds = sb("ds", [P, S], U8)
-        nc.vector.tensor_copy(ds[:].rearrange("p (t m) -> p t m", t=4), ds_got[:].rearrange("p (m t) -> p t m", t=4))
-        for e in range(2):
-            nc.scalar.dma_start(ds[2 + e : P : 32, :].bitcast(I32), ds[16 + e : P : 32, :].bitcast(I32))
-        dw_got = sb("dw_got", [P, S], U32)
-        nc.vector.tensor_copy(dw_got[:], dw_win[:].bitcast(U32).indirect(kidx_t[:]))
-        dw = sb("dw", [P, S], U32)
-        nc.vector.tensor_copy(dw[:].rearrange("p (t m) -> p t m", t=4), dw_got[:].rearrange("p (m t) -> p t m", t=4))
-        xs = sb("xs", [P, S], U8)
-        nc.vector.tensor_copy(xs[:], xs_win[:].indirect(offs_t[:]))
-        xw = sb("xw", [P, S], U32)
-        nc.vector.tensor_copy(xw[:], xw_win[:].bitcast(U32).indirect(offs_t[:]))
+        d_scale_got = sbuf("d_scale_got", [P, S], U8)
+        nc.vector.tensor_copy(d_scale_got[:], d_scale_win[:].indirect(kidx_t[:]))
+        x_scale_got = sbuf("x_scale_got", [P, S], U8)
+        nc.vector.tensor_copy(x_scale_got[:], x_scale_win[:].indirect(offs_t[:]))
+        picked_scales = sbuf("picked_scales", [P, 2 * S], U8)
+        d_scale = picked_scales[:, :S]
+        x_scale = picked_scales[:, S:]
+        nc.vector.tensor_copy(
+            d_scale.rearrange("p (t m) -> p t m", t=TILES), d_scale_got[:].rearrange("p (m t) -> p t m", t=TILES)
+        )
+        nc.vector.tensor_copy(x_scale.bitcast(I32), x_scale_got[:].bitcast(I32))
+        for r in range(1, 4):
+            nc.scalar.dma_start(picked_scales[r:P:32, :].bitcast(I32), picked_scales[8 * r : P : 32, :].bitcast(I32))
+
+        d_word_got = sbuf("d_word_got", [P, S], U32)
+        nc.vector.tensor_copy(d_word_got[:], d_word_win[:].bitcast(U32).indirect(kidx_t[:]))
+        w1_scale_raw = reused.tile([P, S], U8, name="w1_scale_raw", offset=D_WORDS_AT)
+        nc.gpsimd.memset(w1_scale_raw[:].bitcast(I32), 0)
+        for r in range(4):
+            nc.sync.dma_start(w1_scale_raw[r:P:32, :].bitcast(I32), w1_scales[0].bitcast(I32)[r:BLOCKS:4, :])
+        d_word = sbuf("d_word", [P, S], U32)
+        nc.vector.tensor_copy(d_word[:].rearrange("p (t b i) -> p b t i", t=TILES, i=4), interleaved(d_word_got[:]))
+        x_word = sbuf("x_word", [P, S], U32)
+        for lo, hi in HALVES:
+            nc.vector.tensor_copy(x_word[:, lo:hi], x_word_win[:].bitcast(U32).indirect(entries(offs_t, lo, hi)))
 
         tabs = []
-        for t in range(4):
-            tab_t = shared.tile([P, S], F32, name="tab%d" % t, offset=4 * S * t)
-            nc.sync.dma_start(tab_t[:], tab.rearrange("(p t) c -> p t c", t=4)[:, t, :])
+        for t in range(TILES):
+            tab_t = reused.tile([P, S], F32, name="tab%d" % t, offset=TAB_AT + 4 * S * t)
+            nc.sync.dma_start(tab_t[:], tab.rearrange("(p t) c -> p t c", t=TILES)[:, t, :])
             tabs.append(tab_t)
-        ws_raw = shared.tile([P, S], U8, name="ws_raw", offset=4 * T)
-        nc.gpsimd.memset(ws_raw[:].bitcast(I32), 0)
-        for r in range(4):
-            nc.sync.dma_start(ws_raw[r:P:32, :].bitcast(I32), w1_scales[0].bitcast(I32)[r:16:4, :])
 
-        halves = [(0, 256), (256, 512)]
-        den = sb("den", [P, 4, S], F32)
-        num = sb("num", [P, 4, S], F32)
-        g2 = sb("g2", [P, 4], F32)
-        nc.vector.tensor_scalar(g2[:], g_raw[:], 2.0, None, MULT)
-        banks = []
-        for t in range(4):
-            bank = psum.tile([P, S], F32, name="s%d" % t)
-            cols = slice(t * P, (t + 1) * P)
-            nc.tensor.matmul_mx(bank[:], lhsT=dw[:, cols].bitcast(FP8X4), lhsT_scale=ds[:, cols],
-                                rhs=xw[:].bitcast(FP8X4), rhs_scale=xs[:], start=True, stop=True)
-            banks.append(bank)
-        exs = []
-        for t in range(4):
-            ex = sb("ex%d" % t, [P, S], F32)
-            other = sb("other%d" % t, [P, S], F32)
-            nc.scalar.activation(ex[:], banks[t][:], ACT.Exp, scale=0.03125)
-            if t in SCALAR_TILES:
-                nc.scalar.copy(other[:], banks[t][:])
-            else:
-                nc.scalar.activation(other[:], banks[t][:], ACT.Exp, scale=0.03125)
-            exs.append((ex, other))
-        for t in range(4):
-            ex, other = exs[t]
-            part = sb("part%d" % t, [P, S], F32)
-            if t in SCALAR_TILES:
-                e1 = sb("e1_%d" % t, [P, S], F32)
-                e2 = sb("e2_%d" % t, [P, S], F32)
-                for lo, hi in halves:
-                    nc.scalar.activation(e1[:, lo:hi], other[:].indirect(entries(n1_t, lo, hi)), ACT.Exp, scale=0.03125)
-                    nc.scalar.activation(e2[:, lo:hi], other[:].indirect(entries(n2_t, lo, hi)), ACT.Exp, scale=0.03125)
-                    nc.vector.tensor_tensor(part[:, lo:hi], e1[:, lo:hi], ex[:, lo:hi], ADD)
-                    nc.vector.tensor_tensor(den[:, t, lo:hi], part[:, lo:hi], e2[:, lo:hi], ADD)
-            else:
-                for lo, hi in halves:
-                    nc.vector.tensor_tensor(part[:, lo:hi], ex[:].indirect(entries(n1_t, lo, hi)), other[:, lo:hi], ADD)
-                for lo, hi in halves:
-                    nc.vector.tensor_tensor(den[:, t, lo:hi], ex[:].indirect(entries(n2_t, lo, hi)), part[:, lo:hi], ADD)
-            nc.vector.tensor_scalar(num[:, t, :], ex[:], g2[:, t : t + 1], None, MULT)
-
-        ww = sb("ww", [P, 2 * S], U8)
-        nc.vector.tensor_copy(ww[:].rearrange("p (t m b) -> p t m b", t=4, b=2), ww_raw[:].rearrange("p (m t b) -> p t m b", t=4, b=2))
-        ws = sb("ws", [P, S], U8)
-        nc.vector.tensor_copy(ws[:].rearrange("p (t m) -> p t m", t=4), ws_raw[:].rearrange("p (m t) -> p t m", t=4))
-
-        gain = sb("gain", [P, 4, S], F32)
-        for t in range(4):
-            for lo, hi in halves:
-                nc.vector.tensor_copy(gain[:, t, lo:hi], tabs[t][:].indirect(entries(n3_t, lo, hi)))
-
-        hbanks = [psum.tile([P, S], F32, name="h%d" % t) for t in range(4)]
-        zw = sb("zw", [P, S], U32)
-        zs = sb("zs", [P, S], U8)
-        for c in range(4):
-            cols = slice(c * P, (c + 1) * P)
-            root = sb("root%d" % c, [P, 4, P], F32)
-            inv = sb("inv%d" % c, [P, 4, P], F32)
-            nc.scalar.activation(root[:], den[:, :, cols], ACT.Abs_reciprocal_sqrt)
-            nc.scalar.activation(inv[:], root[:], ACT.Square)
-            z = sb("z%d" % c, [P, 4 * P], BF16)
-            nc.vector.tensor_tensor(
-                z[:].rearrange("p (b i t) -> p b t i", i=4, t=4),
-                num[:, :, cols].rearrange("p t (b i) -> p b t i", i=4),
-                inv[:].rearrange("p t (b i) -> p b t i", i=4),
-                MULT,
+        def score(bank, t, lo, hi):
+            keys = slice(t * P, (t + 1) * P)
+            nc.tensor.matmul_mx(
+                bank[:],
+                lhsT=d_word[:, keys].bitcast(FP8X4),
+                lhsT_scale=d_scale[:, keys],
+                rhs=x_word[:, lo:hi].bitcast(FP8X4),
+                rhs_scale=x_scale[:, lo:hi],
+                start=True,
+                stop=True,
             )
-            nc.vector.quantize_mx(out=zw[:, cols].bitcast(FP8X4), scales=zs[:, cols], in_=z[:])
-            for t in range(4):
-                nc.tensor.matmul_mx(hbanks[t][:, cols], lhsT=ww[:, 2 * P * t : 2 * P * (t + 1)].bitcast(FP4X4),
-                                    lhsT_scale=ws[:, P * t : P * (t + 1)], rhs=zw[:, cols].bitcast(FP8X4),
-                                    rhs_scale=zs[:, cols], start=True, stop=True)
-        hs = []
-        for t in range(4):
-            h = sb("hs%d" % t, [P, S], F32)
-            nc.scalar.copy(h[:], hbanks[t][:])
-            hs.append(h)
+            return bank
 
-        ow = sb("ow", [P, S], I32)
-        osc = sb("osc", [P, S], U8)
-        out_rows = out_0.rearrange("(p t) c -> p t c", t=4)
+        parts = [(0, lo, hi, "h%d" % k) for k, (lo, hi) in enumerate(HALVES)]
+        parts = parts + [(t, 0, S, "a%d" % t) for t in range(1, TILES)]
+        scores = [score(psum.tile([P, hi - lo], F32, name="s_" + tag, tag=tag), t, lo, hi) for t, lo, hi, tag in parts]
+        for (t, lo, hi, tag), bank in zip(parts, scores):
+            nc.scalar.activation(ex[t][:, lo:hi], bank[:], ACT.Exp, scale=EXP_SCALE)
+        for (t, lo, hi, tag), bank in zip(parts, scores):
+            if t in SCALAR_TILES:
+                nc.scalar.copy(raw_wins[t][:, :S], bank[:])
+
+        by_n1 = [sbuf("by_n1_%d" % t, [P, S], F32) for t in range(TILES)]
+        by_n2 = [h_wins[t][:, S:] for t in range(TILES)]
+        for t in VECTOR_TILES:
+            nc.vector.tensor_copy(by_n1[t][:], ex_wins[t][:].indirect(n1_t[:]))
+        for t in VECTOR_TILES:
+            nc.vector.tensor_tensor(by_n2[t], ex_wins[t][:].indirect(n2_t[:]), by_n1[t][:], ADD)
+        for t in SCALAR_TILES:
+            nc.scalar.activation(by_n1[t][:], raw_wins[t][:].indirect(n1_t[:]), ACT.Exp, scale=EXP_SCALE)
+            nc.scalar.activation(by_n2[t], raw_wins[t][:].indirect(n2_t[:]), ACT.Exp, scale=EXP_SCALE)
+        terms = [[ex[t], by_n2[t]] for t in VECTOR_TILES] + [[ex[t], by_n1[t][:], by_n2[t]] for t in SCALAR_TILES]
+
+        later = sbuf("later", [P, 2 * TILES, S], F32, tag="by_n1_%d" % VECTOR_TILES[-1])
+        numerator = later[:, :TILES, :]
+        factor = later[:, TILES:, :]
+        for t in range(TILES):
+            nc.vector.tensor_scalar(numerator[:, t, :], ex[t], gain[:, t : t + 1], 2.0, MULT, MULT)
+
+        dens = [psum.tile([P, TILES, P], F32, name="den%d" % c, tag="a%d" % c) for c in range(S // P)]
+        for t in range(TILES):
+            for c, den in enumerate(dens):
+                for k, term in enumerate(terms[t]):
+                    nc.tensor.matmul(
+                        den[:, t, :],
+                        term[:, c * P : (c + 1) * P],
+                        ident[:],
+                        is_transpose=True,
+                        start=(k == 0),
+                        stop=(k == len(terms[t]) - 1),
+                    )
+
+        w1_word = reused.tile([P, 2 * S], U8, name="w1_word", offset=W1_WORDS_AT, align_bytes=64)
+        nc.vector.tensor_copy(
+            w1_word[:].rearrange("p (t m b) -> p t m b", t=TILES, b=2),
+            w1_word_raw[:].rearrange("p (m t b) -> p t m b", t=TILES, b=2),
+        )
+        w1_scale = reused.tile([P, S], U8, name="w1_scale", offset=W1_SCALES_AT, align_bytes=64)
+        nc.vector.tensor_copy(
+            w1_scale[:].rearrange("p (t m) -> p t m", t=TILES), w1_scale_raw[:].rearrange("p (m t) -> p t m", t=TILES)
+        )
+
+        for t in range(TILES):
+            for lo, hi in HALVES:
+                nc.vector.tensor_copy(factor[:, t, lo:hi], tabs[t][:].indirect(entries(n3_t, lo, hi)))
+
+        h_banks = [psum.tile([P, S], F32, name="h%d" % t) for t in range(TILES)]
+        z_word = sbuf("z_word", [P, S], U32)
+        z_scale = sbuf("z_scale", [P, S], U8)
+        for c, den in enumerate(dens):
+            cols = slice(c * P, (c + 1) * P)
+            root = sbuf("root%d" % c, [P, TILES, P], F32)
+            inverse = sbuf("inverse%d" % c, [P, TILES, P], F32)
+            nc.scalar.activation(root[:], den[:], ACT.Abs_reciprocal_sqrt)
+            back = psum.tile([P, TILES, P], F32, name="back%d" % c, tag="a%d" % c)
+            for t in range(TILES):
+                nc.tensor.transpose(back[:, t, :], root[:, t, :], ident[:])
+            nc.scalar.activation(inverse[:], back[:], ACT.Square)
+            z = sbuf("z%d" % c, [P, TILES * P], BF16)
+            nc.vector.tensor_tensor(interleaved(z[:]), by_lines(numerator[:, :, cols]), by_lines(inverse[:]), MULT)
+            nc.vector.quantize_mx(out=z_word[:, cols].bitcast(FP8X4), scales=z_scale[:, cols], in_=z[:])
+            if c % 2:
+                lo, hi = HALVES[c // 2]
+                for t in range(TILES):
+                    nc.tensor.matmul_mx(
+                        h_banks[t][:, lo:hi],
+                        lhsT=w1_word[:, 2 * P * t : 2 * P * (t + 1)].bitcast(FP4X4),
+                        lhsT_scale=w1_scale[:, P * t : P * (t + 1)],
+                        rhs=z_word[:, lo:hi].bitcast(FP8X4),
+                        rhs_scale=z_scale[:, lo:hi],
+                        start=True,
+                        stop=True,
+                    )
+
+        shift = sbuf("shift", [P, S], F32, tag="z%d" % (len(dens) - 1))
+        for lo, hi in HALVES:
+            nc.vector.tensor_copy(shift[:, lo:hi], tabs[0][:].indirect(entries(n4_t, lo, hi)))
+
+        product = sbuf("product", [P, TILES, S], F32)
+        for t in range(TILES):
+            nc.scalar.copy(h_wins[t][:, :S], h_banks[t][:])
+            nc.vector.tensor_tensor(product[:, t, :], h_wins[t][:].indirect(n5_t[:]), factor[:, t, :], MULT)
+
+        out_word = sbuf("out_word", [P, S], I32)
+        out_scale = sbuf("out_scale", [P, S], U8)
+        out_rows = out_0.rearrange("(p t) c -> p t c", t=TILES)
         out_words = out_1[0].rearrange("p n t -> p (n t)").bitcast(I32)
-        for k, (lo, hi) in enumerate([(0, 256), (256, 384), (384, 512)]):
-            n = hi - lo
-            prod = sb("prod%d" % k, [P, 4, n], F32)
-            res = sb("res%d" % k, [P, 4, n], F32)
-            for t in range(4):
-                nc.vector.tensor_tensor(prod[:, t, :], hs[t][:].indirect(entries(n5_t, lo, hi)), gain[:, t, lo:hi], MULT)
-            for t in range(4):
-                nc.vector.tensor_tensor(res[:, t, :], tabs[t][:].indirect(entries(n4_t, lo, hi)), prod[:, t, :], ADD)
-            nc.sync.dma_start(out_rows[:, :, lo:hi], res[:])
-            rb = sb("rb%d" % k, [P, 4 * n], BF16)
-            nc.scalar.copy(rb[:].rearrange("p (b i t) -> p b t i", i=4, t=4), res[:].rearrange("p t (b i) -> p b t i", i=4))
-            nc.vector.quantize_mx(out=ow[:, lo:hi].bitcast(FP8X4), scales=osc[:, lo:hi], in_=rb[:])
-            nc.sync.dma_start(out_words[:, lo:hi], ow[:, lo:hi])
+        for k, (lo, hi) in enumerate(OUT_CHUNKS):
+            result = sbuf("result%d" % k, [P, TILES, hi - lo], F32)
+            nc.vector.tensor_tensor(result[:, 0, :], shift[:, lo:hi], product[:, 0, lo:hi], ADD)
+            for t in range(1, TILES):
+                nc.vector.tensor_tensor(
+                    result[:, t, :], tabs[t][:].indirect(entries(n4_t, lo, hi)), product[:, t, lo:hi], ADD
+                )
+            nc.sync.dma_start(out_rows[:, :, lo:hi], result[:])
+            rounded = sbuf("rounded%d" % k, [P, TILES * (hi - lo)], BF16)
+            round_copy = nc.vector.tensor_copy if hi == S else nc.scalar.copy
+            round_copy(interleaved(rounded[:]), by_lines(result[:]))
+            nc.vector.quantize_mx(out=out_word[:, lo:hi].bitcast(FP8X4), scales=out_scale[:, lo:hi], in_=rounded[:])
+            nc.sync.dma_start(out_words[:, lo:hi], out_word[:, lo:hi])
         for r in range(4):
             queue = nc.scalar if r % 2 else nc.sync
-            queue.dma_start(out_2[0].bitcast(I32)[r:16:4, :], osc[r:P:32, :].bitcast(I32))
+            queue.dma_start(out_2[0].bitcast(I32)[r:BLOCKS:4, :], out_scale[r:P:32, :].bitcast(I32))

from contextlib import ExitStack

import concourse.mybir as mybir
from concourse.masks import make_identity

F32 = mybir.dt.float32
BF16 = mybir.dt.bfloat16
I32 = mybir.dt.int32
U32 = mybir.dt.uint32
U16 = mybir.dt.uint16
U8 = mybir.dt.uint8
FP8X4 = mybir.dt.float8_e4m3fn_x4
FP4X4 = mybir.dt.float4_e2m1fn_x4
ACT = mybir.ActivationFunctionType
MULT = mybir.AluOpType.mult
ADD = mybir.AluOpType.add

P = 128
TILES = 4
TABLE = 2048
S = 512
BLOCKS = 16
FLOPS = 2 * 2 * S * S * S
EXP_SCALE = 0.0625 * 0.5
HALVES = ((0, S // 2), (S // 2, S))
VECTOR_TILES = (0, 1)
SCALAR_TILES = (2, 3)
OUT_CHUNKS = ((0, 256), (256, 384), (384, 512))
D_WORDS_AT = 0
X_WORDS_AT = 4 * TABLE
W1_SCALES_AT = 8 * TABLE - S
W1_WORDS_AT = W1_SCALES_AT - 2 * S
TAB_AT = W1_WORDS_AT - TILES * 4 * S


def tile_picked_keysharekinda_none_po_kernel(
    tc, x_words, x_scales, d_words, d_scales, gn, w1_words, w1_scales, tab, offs, kidx, n1, n2, n3, n4, n5, out_0, out_1, out_2
):
    nc = tc.nc
    with ExitStack() as ctx:
        keep = ctx.enter_context(tc.tile_pool(name="keep", bufs=1))
        reused = ctx.enter_context(tc.tile_pool(name="reused", bufs=1))
        psum = ctx.enter_context(tc.psum_pool(name="psum", bufs=1))

        def sbuf(name, shape, dtype, tag=None):
            return keep.tile(shape, dtype, name=name, tag=tag or name, align_bytes=64)

        def load_list(name, src):
            lst = sbuf(name, [P, S // 16], U16)
            nc.sync.dma_start(lst[:], src)
            return lst

        def entries(lst, lo, hi):
            return lst[:, lo // 16 : hi // 16]

        def load_scale_table(name, scales):
            win = sbuf(name, [P, TABLE], U8)
            rows = scales[0].bitcast(I32).unsqueeze(1).to_broadcast([BLOCKS, P // BLOCKS, TABLE // 4])
            nc.sync.dma_start(win[:].bitcast(I32), rows)
            return win

        def load_word_table(name, words, at):
            win = reused.tile([P, TABLE], I32, name=name, offset=at)
            nc.sync.dma_start(win[:], words[0].rearrange("p n t -> p (n t)").bitcast(I32))
            return win

        def by_lines(tiles):
            return tiles.rearrange("p t (b i) -> p b t i", i=4)

        def interleaved(flat):
            return flat.rearrange("p (b i t) -> p b t i", i=4, t=TILES)

        ex_wins = [sbuf("ex_win%d" % t, [P, 2 * S], F32) for t in VECTOR_TILES]
        nc.vector.memset(ex_wins[0][:, S:], 0.0)
        nc.scalar.activation(ex_wins[1][:, S:], ex_wins[0][:, S:], ACT.Exp)
        raw_wins = {t: sbuf("raw_win%d" % t, [P, 2 * S], F32) for t in SCALAR_TILES}
        h_wins = [sbuf("h_win%d" % t, [P, 2 * S], F32) for t in range(TILES)]
        ex = [ex_wins[t][:, :S] for t in VECTOR_TILES] + [raw_wins[t][:, S:] for t in SCALAR_TILES]
        ident = sbuf("ident", [P, P], F32)
        make_identity(nc, ident[:])

        kidx_t = load_list("kidx_t", kidx)
        d_scale_win = load_scale_table("d_scale_win", d_scales)
        offs_t = load_list("offs_t", offs)
        x_scale_win = load_scale_table("x_scale_win", x_scales)
        n1_t = load_list("n1_t", n1)
        n2_t = load_list("n2_t", n2)
        d_word_win = load_word_table("d_word_win", d_words, D_WORDS_AT)
        x_word_win = load_word_table("x_word_win", x_words, X_WORDS_AT)
        n3_t = load_list("n3_t", n3)
        n5_t = load_list("n5_t", n5)
        n4_t = load_list("n4_t", n4)
        gain = sbuf("gain", [P, TILES], F32)
        nc.sync.dma_start(gain[:], gn.rearrange("(p t) o -> p (t o)", t=TILES))
        w1_word_raw = sbuf("w1_word_raw", [P, 2 * S], U8)
        nc.gpsimd.dma_start(w1_word_raw[:].bitcast(I32), w1_words[0].bitcast(I32))

        d_scale_got = sbuf("d_scale_got", [P, S], U8)
        nc.vector.tensor_copy(d_scale_got[:], d_scale_win[:].indirect(kidx_t[:]))
        x_scale_got = sbuf("x_scale_got", [P, S], U8)
        nc.vector.tensor_copy(x_scale_got[:], x_scale_win[:].indirect(offs_t[:]))
        picked_scales = sbuf("picked_scales", [P, 2 * S], U8)
        d_scale = picked_scales[:, :S]
        x_scale = picked_scales[:, S:]
        nc.vector.tensor_copy(
            d_scale.rearrange("p (t m) -> p t m", t=TILES), d_scale_got[:].rearrange("p (m t) -> p t m", t=TILES)
        )
        nc.vector.tensor_copy(x_scale.bitcast(I32), x_scale_got[:].bitcast(I32))
        for r in range(1, 4):
            nc.scalar.dma_start(picked_scales[r:P:32, :].bitcast(I32), picked_scales[8 * r : P : 32, :].bitcast(I32))

        d_word_got = sbuf("d_word_got", [P, S], U32)
        nc.vector.tensor_copy(d_word_got[:], d_word_win[:].bitcast(U32).indirect(kidx_t[:]))
        w1_scale_raw = reused.tile([P, S], U8, name="w1_scale_raw", offset=D_WORDS_AT)
        nc.gpsimd.memset(w1_scale_raw[:].bitcast(I32), 0)
        for r in range(4):
            nc.sync.dma_start(w1_scale_raw[r:P:32, :].bitcast(I32), w1_scales[0].bitcast(I32)[r:BLOCKS:4, :])
        d_word = sbuf("d_word", [P, S], U32)
        nc.vector.tensor_copy(d_word[:].rearrange("p (t b i) -> p b t i", t=TILES, i=4), interleaved(d_word_got[:]))
        x_word = sbuf("x_word", [P, S], U32)
        for lo, hi in HALVES:
            nc.vector.tensor_copy(x_word[:, lo:hi], x_word_win[:].bitcast(U32).indirect(entries(offs_t, lo, hi)))

        tabs = []
        for t in range(TILES):
            tab_t = reused.tile([P, S], F32, name="tab%d" % t, offset=TAB_AT + 4 * S * t)
            nc.sync.dma_start(tab_t[:], tab.rearrange("(p t) c -> p t c", t=TILES)[:, t, :])
            tabs.append(tab_t)

        def score(bank, t, lo, hi):
            keys = slice(t * P, (t + 1) * P)
            nc.tensor.matmul_mx(
                bank[:],
                lhsT=d_word[:, keys].bitcast(FP8X4),
                lhsT_scale=d_scale[:, keys],
                rhs=x_word[:, lo:hi].bitcast(FP8X4),
                rhs_scale=x_scale[:, lo:hi],
                start=True,
                stop=True,
            )
            return bank

        parts = [(0, lo, hi, "h%d" % k) for k, (lo, hi) in enumerate(HALVES)]
        parts = parts + [(t, 0, S, "a%d" % t) for t in range(1, TILES)]
        scores = [score(psum.tile([P, hi - lo], F32, name="s_" + tag, tag=tag), t, lo, hi) for t, lo, hi, tag in parts]
        for (t, lo, hi, tag), bank in zip(parts, scores):
            nc.scalar.activation(ex[t][:, lo:hi], bank[:], ACT.Exp, scale=EXP_SCALE)
        for (t, lo, hi, tag), bank in zip(parts, scores):
            if t in SCALAR_TILES:
                nc.scalar.copy(raw_wins[t][:, :S], bank[:])

        by_n1 = [sbuf("by_n1_%d" % t, [P, S], F32) for t in range(TILES)]
        by_n2 = [h_wins[t][:, S:] for t in range(TILES)]
        for t in VECTOR_TILES:
            nc.vector.tensor_copy(by_n1[t][:], ex_wins[t][:].indirect(n1_t[:]))
        for t in VECTOR_TILES:
            nc.vector.tensor_tensor(by_n2[t], ex_wins[t][:].indirect(n2_t[:]), by_n1[t][:], ADD)
        for t in SCALAR_TILES:
            nc.scalar.activation(by_n1[t][:], raw_wins[t][:].indirect(n1_t[:]), ACT.Exp, scale=EXP_SCALE)
            nc.scalar.activation(by_n2[t], raw_wins[t][:].indirect(n2_t[:]), ACT.Exp, scale=EXP_SCALE)
        terms = [[ex[t], by_n2[t]] for t in VECTOR_TILES] + [[ex[t], by_n1[t][:], by_n2[t]] for t in SCALAR_TILES]

        later = sbuf("later", [P, 2 * TILES, S], F32, tag="by_n1_%d" % VECTOR_TILES[-1])
        numerator = later[:, :TILES, :]
        factor = later[:, TILES:, :]
        for t in range(TILES):
            nc.vector.tensor_scalar(numerator[:, t, :], ex[t], gain[:, t : t + 1], 2.0, MULT, MULT)

        dens = [psum.tile([P, TILES, P], F32, name="den%d" % c, tag="a%d" % c) for c in range(S // P)]
        for t in range(TILES):
            for c, den in enumerate(dens):
                for k, term in enumerate(terms[t]):
                    nc.tensor.matmul(
                        den[:, t, :],
                        term[:, c * P : (c + 1) * P],
                        ident[:],
                        is_transpose=True,
                        start=(k == 0),
                        stop=(k == len(terms[t]) - 1),
                    )

        w1_word = reused.tile([P, 2 * S], U8, name="w1_word", offset=W1_WORDS_AT, align_bytes=64)
        nc.vector.tensor_copy(
            w1_word[:].rearrange("p (t m b) -> p t m b", t=TILES, b=2),
            w1_word_raw[:].rearrange("p (m t b) -> p t m b", t=TILES, b=2),
        )
        w1_scale = reused.tile([P, S], U8, name="w1_scale", offset=W1_SCALES_AT, align_bytes=64)
        nc.vector.tensor_copy(
            w1_scale[:].rearrange("p (t m) -> p t m", t=TILES), w1_scale_raw[:].rearrange("p (m t) -> p t m", t=TILES)
        )

        for t in range(TILES):
            for lo, hi in HALVES:
                nc.vector.tensor_copy(factor[:, t, lo:hi], tabs[t][:].indirect(entries(n3_t, lo, hi)))

        h_banks = [psum.tile([P, S], F32, name="h%d" % t) for t in range(TILES)]
        z_word = sbuf("z_word", [P, S], U32)
        z_scale = sbuf("z_scale", [P, S], U8)
        for c, den in enumerate(dens):
            cols = slice(c * P, (c + 1) * P)
            root = sbuf("root%d" % c, [P, TILES, P], F32)
            inverse = sbuf("inverse%d" % c, [P, TILES, P], F32)
            nc.scalar.activation(root[:], den[:], ACT.Abs_reciprocal_sqrt)
            back = psum.tile([P, TILES, P], F32, name="back%d" % c, tag="a%d" % c)
            for t in range(TILES):
                nc.tensor.transpose(back[:, t, :], root[:, t, :], ident[:])
            nc.scalar.activation(inverse[:], back[:], ACT.Square)
            z = sbuf("z%d" % c, [P, TILES * P], BF16)
            nc.vector.tensor_tensor(interleaved(z[:]), by_lines(numerator[:, :, cols]), by_lines(inverse[:]), MULT)
            nc.vector.quantize_mx(out=z_word[:, cols].bitcast(FP8X4), scales=z_scale[:, cols], in_=z[:])
            if c % 2:
                lo, hi = HALVES[c // 2]
                for t in range(TILES):
                    nc.tensor.matmul_mx(
                        h_banks[t][:, lo:hi],
                        lhsT=w1_word[:, 2 * P * t : 2 * P * (t + 1)].bitcast(FP4X4),
                        lhsT_scale=w1_scale[:, P * t : P * (t + 1)],
                        rhs=z_word[:, lo:hi].bitcast(FP8X4),
                        rhs_scale=z_scale[:, lo:hi],
                        start=True,
                        stop=True,
                    )

        shift = sbuf("shift", [P, S], F32, tag="z%d" % (len(dens) - 1))
        for lo, hi in HALVES:
            nc.vector.tensor_copy(shift[:, lo:hi], tabs[0][:].indirect(entries(n4_t, lo, hi)))

        product = sbuf("product", [P, TILES, S], F32)
        for t in range(TILES):
            nc.scalar.copy(h_wins[t][:, :S], h_banks[t][:])
            nc.vector.tensor_tensor(product[:, t, :], h_wins[t][:].indirect(n5_t[:]), factor[:, t, :], MULT)

        out_word = sbuf("out_word", [P, S], I32)
        out_scale = sbuf("out_scale", [P, S], U8)
        out_rows = out_0.rearrange("(p t) c -> p t c", t=TILES)
        out_words = out_1[0].rearrange("p n t -> p (n t)").bitcast(I32)
        for k, (lo, hi) in enumerate(OUT_CHUNKS):
            result = sbuf("result%d" % k, [P, TILES, hi - lo], F32)
            nc.vector.tensor_tensor(result[:, 0, :], shift[:, lo:hi], product[:, 0, lo:hi], ADD)
            for t in range(1, TILES):
                nc.vector.tensor_tensor(
                    result[:, t, :], tabs[t][:].indirect(entries(n4_t, lo, hi)), product[:, t, lo:hi], ADD
                )
            nc.sync.dma_start(out_rows[:, :, lo:hi], result[:])
            rounded = sbuf("rounded%d" % k, [P, TILES * (hi - lo)], BF16)
            round_copy = nc.vector.tensor_copy if hi == S else nc.scalar.copy
            round_copy(interleaved(rounded[:]), by_lines(result[:]))
            nc.vector.quantize_mx(out=out_word[:, lo:hi].bitcast(FP8X4), scales=out_scale[:, lo:hi], in_=rounded[:])
            nc.sync.dma_start(out_words[:, lo:hi], out_word[:, lo:hi])
        for r in range(4):
            queue = nc.scalar if r % 2 else nc.sync
            queue.dma_start(out_2[0].bitcast(I32)[r:BLOCKS:4, :], out_scale[r:P:32, :].bitcast(I32))
